import numpy as np
import ml_dtypes


def mxq(x, axis, fmt="e4m3"):
    dtype, down = {"e4m3": (ml_dtypes.float8_e4m3fn, 7), "e5m2": (ml_dtypes.float8_e5m2, 14)}[fmt]
    v = np.moveaxis(np.asarray(x, np.float32).astype(ml_dtypes.bfloat16).astype(np.float64), axis, -1)
    blocks = v.reshape(v.shape[:-1] + (-1, 32))
    amax = np.abs(blocks).max(-1, keepdims=True)
    byte = np.maximum(np.where(amax > 0, np.frexp(amax)[1] - 1 + 127, 0) - down, 1)
    scale = np.exp2(byte - 127.0)
    codes = (blocks / scale).astype(np.float32).astype(dtype).astype(np.float64)
    return np.moveaxis((codes * scale).reshape(v.shape), -1, axis)


WIDE = False


def mx_kscale(k):
    if not WIDE:
        return np.ones(k)
    levels = np.array([10, -10, 5, -5, 0])
    if k % 512:
        return np.exp2(np.random.permutation(np.resize(levels, k // 32))).repeat(32)
    a = np.empty((k // 512, 16))
    for p in range(k // 512):
        a[p, :8] = np.random.permutation(np.resize(levels, 8))
        for g in range(8):
            far = levels[np.abs(levels - a[p, g]) >= 10]
            a[p, g + 8] = far[np.random.randint(len(far))]
    return np.exp2(a.ravel()).repeat(32)


def f64(x):
    return np.asarray(x).astype(np.float64)


def striped(idx):
    return np.tile(idx.reshape(-1, 16).T, (8, 1)).astype(np.uint16)


def unstriped(offs):
    return offs[:16].T.reshape(-1).astype(np.int64)


E2M1 = np.array([0.0, 0.5, 1.0, 1.5, 2.0, 3.0, 4.0, 6.0, -0.0, -0.5, -1.0, -1.5, -2.0, -3.0, -4.0, -6.0])


def pack_weight(w, fmt):
    k, n = w.shape
    w = f64(np.asarray(w, np.float32).astype(ml_dtypes.bfloat16)).reshape(k // 32, 32, n)
    amax = np.abs(w).max(1)
    if fmt == "e4m3":
        byte = np.frexp(amax)[1] - 1 + 127 - 7
    else:
        mant, ex = np.frexp(amax / 6.0)
        byte = np.where(mant > 0.5, ex, ex - 1) + 127
    byte = np.clip(np.where(amax > 0, byte, 1), 1, 254)
    scaled = (w * np.exp2(127.0 - byte)[:, None, :]).reshape(k, n).astype(np.float32)
    by_word = np.ascontiguousarray(scaled.reshape(k // 512, 128, 4, n).transpose(0, 1, 3, 2))
    if fmt == "e4m3":
        words = by_word.astype(ml_dtypes.float8_e4m3fn).view(np.uint8)
    else:
        c = by_word.astype(ml_dtypes.float4_e2m1fn).view(np.uint8) & 0xF
        words = (c[..., 0::2] | (c[..., 1::2] << 4)).reshape(k // 512, 128, 2 * n)
    return np.ascontiguousarray(words), np.ascontiguousarray(byte.astype(np.uint8).reshape(k // 512, 16, n))


def unpack_weight(words, scales, fmt):
    g, _, n = scales.shape
    words = np.ascontiguousarray(words).reshape(g, 128, n, -1)
    if fmt == "e4m3":
        vals = words.view(ml_dtypes.float8_e4m3fn).astype(np.float64)
    else:
        nib = np.empty((g, 128, n, 4), np.uint8)
        nib[..., 0::2] = words & 0xF
        nib[..., 1::2] = words >> 4
        vals = E2M1[nib]
    vals = vals * np.repeat(np.exp2(scales.astype(np.float64) - 127.0), 8, axis=1)[..., None]
    return vals.transpose(0, 1, 3, 2).reshape(g * 512, n)


def silu(v):
    return v / (1.0 + np.exp(-np.maximum(v, -700.0)))


K, T, E, C, N = 1024, 640, 20, 128, 256
TOP = 4


def by_expert(wq, xq):
    return np.concatenate([wq[e].T @ xq[:, e * C:(e + 1) * C] for e in range(E)], axis=1)


def setup_inputs():
    n = np.random.standard_normal
    s = mx_kscale(K)[:, None]
    deal = np.repeat(np.arange(E), C).reshape(TOP, T)[:, np.random.permutation(T)]
    deal = np.take_along_axis(deal, np.argsort(np.random.rand(TOP, T), axis=0), axis=0)
    for _ in range(8):
        s_, t_ = np.random.permutation(T).reshape(2, -1); r = np.random.randint(TOP, size=T // 2); x, y = deal[r, s_].copy(), deal[r, t_].copy()
        ok = ~((deal[:, s_] == y).any(0) | (deal[:, t_] == x).any(0)); deal[r[ok], s_[ok]] = y[ok]; deal[r[ok], t_[ok]] = x[ok]
    order = np.lexsort((np.random.rand(TOP * T), deal.reshape(-1)))
    slot_token = order % T; pos = np.empty(TOP * T, np.int64); pos[order] = np.arange(TOP * T); pos = pos.reshape(TOP, T)
    g = np.random.uniform(0.5, 1.5, (TOP, T)); g = g / g.sum(0)
    x = pack_weight(n((K, T)) * s, "e4m3")
    return {
        "x_words": x[0],
        "x_scales": x[1],
        "w": (n((E, K, N)) / np.sqrt(K) / s[None]).astype(np.float32),
        "b": (0.3 * n((N, E))).astype(np.float32),
        "gate": np.stack([np.tile(r, (N, 1)) for r in g]).astype(np.float32),
        "offs": striped(slot_token),
        "pos1": striped(pos[0]),
        "pos2": striped(pos[1]),
        "pos3": striped(pos[2]),
        "pos4": striped(pos[3]),
    }


def reference(x_words, x_scales, w, b, gate, offs, pos1, pos2, pos3, pos4):
    idx = unstriped(offs)
    xq = unpack_weight(x_words, x_scales, "e4m3")[:, idx]
    y = by_expert(mxq(f64(w), 1, "e4m3"), xq)
    y = silu(y + np.repeat(f64(b), C, axis=1))
    return sum(f64(gate[r]) * y[:, unstriped(p)] for r, p in enumerate((pos1, pos2, pos3, pos4)))

@@ -1,0 +1,189 @@
+from contextlib import ExitStack
+
+import concourse.mybir as mybir
+
+K, T, E, C, N = 1024, 640, 20, 128, 256
+TOP = 4
+S = E * C
+FLOPS = 2 * S * K * N
+
+F32 = mybir.dt.float32
+BF16 = mybir.dt.bfloat16
+I32 = mybir.dt.int32
+U32 = mybir.dt.uint32
+U16 = mybir.dt.uint16
+U8 = mybir.dt.uint8
+FP8X4 = mybir.dt.float8_e4m3fn_x4
+MULT = mybir.AluOpType.mult
+ADD = mybir.AluOpType.add
+SILU = mybir.ActivationFunctionType.Silu
+
+P = 128
+PACK = 4
+PASSES = K // (P * PACK)
+HALVES = N // P
+WINDOW = 896
+PIECE = 640
+RAW_BUFS = 12
+SCALAR_N = 64
+
+
+def tile_moe_pkd_lin_silu_kernel(
+    tc, x_words, x_scales, w, b, gate, offs, pos1, pos2, pos3, pos4, out
+):
+    nc = tc.nc
+    with ExitStack() as ctx:
+        keep = ctx.enter_context(tc.tile_pool(name="keep", bufs=1))
+        stream = ctx.enter_context(tc.tile_pool(name="stream", bufs=RAW_BUFS))
+        stage = ctx.enter_context(tc.tile_pool(name="stage", bufs=4))
+        psum = ctx.enter_context(tc.psum_pool(name="psum", bufs=6))
+
+        slot_list = keep.tile([P, S // 16], U16, name="slot_list")
+        nc.sync.dma_start(slot_list[:], offs)
+
+        token_words = []
+        for o in range(PASSES):
+            words = keep.tile([P, WINDOW], I32, name=f"token_words{o}", align_bytes=64)
+            nc.vector.memset(words[:, T:], 0)
+            nc.sync.dma_start(words[:, :T], x_words[o].rearrange("p t r -> p (t r)").bitcast(I32))
+            token_words.append(words)
+
+        token_scales = keep.tile([P, WINDOW], U8, name="token_scales", align_bytes=64)
+        nc.gpsimd.memset(token_scales[:], 0)
+        for q in range(4):
+            nc.scalar.dma_start(
+                token_scales[32 * q : 32 * q + 4 * PASSES, :T].bitcast(I32),
+                x_scales[:, 4 * q : 4 * q + 4, :].bitcast(I32),
+            )
+        bias = keep.tile([P, HALVES, 32], F32, name="bias")
+        nc.scalar.dma_start(bias[:, :, :E], b.rearrange("(h p) e -> p h e", p=P))
+
+        slot_words = [keep.tile([P, S], U32, name=f"slot_words{o}", align_bytes=64) for o in range(PASSES)]
+        slot_scales = keep.tile([P, S], U8, name="slot_scales", align_bytes=64)
+        y = [keep.tile([P, S], F32, name=f"y{h}", align_bytes=64) for h in range(HALVES)]
+
+        def gather_tokens(piece, sort):
+            cols = slice(piece * PIECE, (piece + 1) * PIECE)
+            offsets = slot_list[:, piece * PIECE // 16 : (piece + 1) * PIECE // 16]
+            if sort < PASSES:
+                nc.vector.tensor_copy(slot_words[sort][:, cols], token_words[sort][:].bitcast(U32).indirect(offsets))
+            else:
+                nc.vector.tensor_copy(slot_scales[:, cols], token_scales[:].indirect(offsets))
+
+        def interleave(copy, grouped, raw, n0, n1):
+            copy(
+                grouped[:, n0:n1, :].rearrange("p (c i) t -> p c t i", i=4),
+                raw[:, :, n0:n1].rearrange("p t (c i) -> p c t i", i=4),
+            )
+
+        def quantize(codes, scales, grouped, lo, hi):
+            nc.vector.quantize_mx(
+                out=codes[:, lo:hi].bitcast(FP8X4),
+                scales=scales[:, lo:hi],
+                in_=grouped[:].rearrange("p o n t -> p (o n t)")[:, PACK * lo : PACK * hi],
+            )
+
+        def multiply(e, h, codes, scales):
+            cols = slice(e * C, (e + 1) * C)
+            acc = psum.tile([P, C], F32, name="acc")
+            for o in range(PASSES):
+                m = slice(o * N + h * P, o * N + (h + 1) * P)
+                nc.tensor.matmul_mx(
+                    out=acc[:],
+                    lhsT=codes[:, m].bitcast(FP8X4),
+                    lhsT_scale=scales[:, m],
+                    rhs=slot_words[o][:, cols].bitcast(FP8X4),
+                    rhs_scale=slot_scales[4 * o :, cols],
+                    start=(o == 0),
+                    stop=(o == PASSES - 1),
+                )
+            nc.scalar.activation(y[h][:, cols], acc[:], SILU, bias=bias[:, h, e : e + 1])
+
+        for sort in range(PASSES + 1):
+            gather_tokens(0, sort)
+
+        per_piece = PIECE // C
+        pending = None
+        for e in range(E):
+            last = e == E - 1
+            rows = w[e].rearrange("(o p t) n -> p o t n", p=P, t=PACK)
+            if last:
+                raw = []
+                for o in range(PASSES):
+                    part = stream.tile([P, PACK, N], F32, name="raw")
+                    nc.sync.dma_start(part[:], rows[:, o])
+                    raw.append(part[:])
+            else:
+                both = stream.tile([P, PASSES, PACK, N], F32, name="raw")
+                nc.sync.dma_start(both[:], rows)
+                raw = [both[:, o] for o in range(PASSES)]
+            grouped = stage.tile([P, PASSES, N, PACK], BF16, name="grouped", align_bytes=64)
+            codes = stage.tile([P, PASSES * N], U32, name="codes", align_bytes=64)
+            scales = stage.tile([P, PASSES * N], U8, name="scales", align_bytes=64)
+            interleave(nc.scalar.copy, grouped[:, 0], raw[0], 0, N)
+            if last:
+                if pending is not None:
+                    pending()
+                quantize(codes, scales, grouped, 0, N)
+                interleave(nc.vector.tensor_copy, grouped[:, 1], raw[1], 0, P)
+                interleave(nc.scalar.copy, grouped[:, 1], raw[1], P, N)
+                for h in range(HALVES):
+                    quantize(codes, scales, grouped, N + h * P, N + (h + 1) * P)
+                    multiply(e, h, codes, scales)
+            else:
+                interleave(nc.scalar.copy, grouped[:, 1], raw[1], 0, SCALAR_N)
+                interleave(nc.vector.tensor_copy, grouped[:, 1], raw[1], SCALAR_N, N)
+                if pending is not None:
+                    pending()
+
+                def finish(e=e, codes=codes, scales=scales, grouped=grouped):
+                    quantize(codes, scales, grouped, 0, PASSES * N)
+                    for h in range(HALVES):
+                        multiply(e, h, codes, scales)
+
+                pending = finish
+                piece, step = divmod(e, per_piece)
+                if piece + 1 < S // PIECE and step <= PASSES:
+                    gather_tokens(piece + 1, step)
+
+        token_lists = []
+        for r, pos in enumerate((pos1, pos2, pos3, pos4)):
+            one = keep.tile([P, T // 16], U16, name=f"token_list{r}")
+            nc.sync.dma_start(one[:], pos)
+            token_lists.append(one)
+
+        gates = {}
+        for h in range(HALVES):
+            for pair in range(TOP // 2):
+                g = stream.tile([P, 2, T], F32, name="raw")
+                nc.sync.dma_start(
+                    g[:], gate[2 * pair : 2 * pair + 2, h * P : (h + 1) * P, :].rearrange("r p t -> p r t")
+                )
+                gates[(h, 2 * pair)] = g[:, 0]
+                gates[(h, 2 * pair + 1)] = g[:, 1]
+
+        cut = T // 2
+        for h in range(HALVES):
+            terms = [keep.tile([P, T], F32, name=f"term{h}_{r}") for r in range(TOP)]
+            sum01 = keep.tile([P, T], F32, name=f"sum01_{h}")
+            sum012 = keep.tile([P, T], F32, name=f"sum012_{h}")
+            total = keep.tile([P, T], F32, name=f"total{h}")
+
+            def fetch(r, t0, t1):
+                nc.vector.tensor_tensor(
+                    terms[r][:, t0:t1],
+                    y[h][:].indirect(token_lists[r][:, t0 // 16 : t1 // 16]),
+                    gates[(h, r)][:, t0:t1],
+                    MULT,
+                )
+
+            fetch(0, 0, T)
+            fetch(1, 0, T)
+            fetch(2, 0, T)
+            nc.vector.tensor_tensor(sum01[:], terms[0][:], terms[1][:], ADD)
+            fetch(3, 0, cut)
+            nc.vector.tensor_tensor(sum012[:], sum01[:], terms[2][:], ADD)
+            fetch(3, cut, T)
+            for t0, t1 in ((0, cut), (cut, T)):
+                nc.vector.tensor_tensor(total[:, t0:t1], sum012[:, t0:t1], terms[3][:, t0:t1], ADD)
+                nc.sync.dma_start(out[h * P : (h + 1) * P, t0:t1], total[:, t0:t1])

@@ -24,8 +24,11 @@ PASSES = K // (P * PACK)
 HALVES = N // P
 WINDOW = 896
 PIECE = 640
-RAW_BUFS = 12
-SCALAR_N = 64
+RAW_BUFS = 10
+GROUPED_BUFS = 9
+BIAS_AFTER = 6
+SCALAR_ALONE = 6
+SCALAR_N = 32
 
 
 def tile_moe_pkd_lin_silu_kernel(
@@ -35,8 +38,8 @@ def tile_moe_pkd_lin_silu_kernel(
     with ExitStack() as ctx:
         keep = ctx.enter_context(tc.tile_pool(name="keep", bufs=1))
         stream = ctx.enter_context(tc.tile_pool(name="stream", bufs=RAW_BUFS))
-        stage = ctx.enter_context(tc.tile_pool(name="stage", bufs=4))
-        psum = ctx.enter_context(tc.psum_pool(name="psum", bufs=6))
+        stage = ctx.enter_context(tc.tile_pool(name="stage", bufs=GROUPED_BUFS))
+        psum = ctx.enter_context(tc.psum_pool(name="psum", bufs=8))
 
         slot_list = keep.tile([P, S // 16], U16, name="slot_list")
         nc.sync.dma_start(slot_list[:], offs)
@@ -48,15 +51,14 @@ def tile_moe_pkd_lin_silu_kernel(
             nc.sync.dma_start(words[:, :T], x_words[o].rearrange("p t r -> p (t r)").bitcast(I32))
             token_words.append(words)
 
-        token_scales = keep.tile([P, WINDOW], U8, name="token_scales", align_bytes=64)
-        nc.gpsimd.memset(token_scales[:], 0)
+        token_scales = keep.tile([P, WINDOW // 4], I32, name="token_scales", align_bytes=64)
+        nc.vector.memset(token_scales[:], 0)
         for q in range(4):
             nc.scalar.dma_start(
-                token_scales[32 * q : 32 * q + 4 * PASSES, :T].bitcast(I32),
+                token_scales[32 * q : 32 * q + 4 * PASSES, : T // 4],
                 x_scales[:, 4 * q : 4 * q + 4, :].bitcast(I32),
             )
         bias = keep.tile([P, HALVES, 32], F32, name="bias")
-        nc.scalar.dma_start(bias[:, :, :E], b.rearrange("(h p) e -> p h e", p=P))
 
         slot_words = [keep.tile([P, S], U32, name=f"slot_words{o}", align_bytes=64) for o in range(PASSES)]
         slot_scales = keep.tile([P, S], U8, name="slot_scales", align_bytes=64)
@@ -68,7 +70,7 @@ def tile_moe_pkd_lin_silu_kernel(
             if sort < PASSES:
                 nc.vector.tensor_copy(slot_words[sort][:, cols], token_words[sort][:].bitcast(U32).indirect(offsets))
             else:
-                nc.vector.tensor_copy(slot_scales[:, cols], token_scales[:].indirect(offsets))
+                nc.vector.tensor_copy(slot_scales[:, cols], token_scales[:].bitcast(U8).indirect(offsets))
 
         def interleave(copy, grouped, raw, n0, n1):
             copy(
@@ -83,40 +85,48 @@ def tile_moe_pkd_lin_silu_kernel(
                 in_=grouped[:].rearrange("p o n t -> p (o n t)")[:, PACK * lo : PACK * hi],
             )
 
-        def multiply(e, h, codes, scales):
+        def multiply(e, halves, codes, scales):
             cols = slice(e * C, (e + 1) * C)
-            acc = psum.tile([P, C], F32, name="acc")
-            for o in range(PASSES):
-                m = slice(o * N + h * P, o * N + (h + 1) * P)
-                nc.tensor.matmul_mx(
-                    out=acc[:],
-                    lhsT=codes[:, m].bitcast(FP8X4),
-                    lhsT_scale=scales[:, m],
-                    rhs=slot_words[o][:, cols].bitcast(FP8X4),
-                    rhs_scale=slot_scales[4 * o :, cols],
-                    start=(o == 0),
-                    stop=(o == PASSES - 1),
-                )
-            nc.scalar.activation(y[h][:, cols], acc[:], SILU, bias=bias[:, h, e : e + 1])
+            acc = psum.tile([P, len(halves), C], F32, name="acc")
+            for j, h in enumerate(halves):
+                for o in range(PASSES):
+                    m = slice(o * N + h * P, o * N + (h + 1) * P)
+                    nc.tensor.matmul_mx(
+                        out=acc[:, j],
+                        lhsT=codes[:, m].bitcast(FP8X4),
+                        lhsT_scale=scales[:, m],
+                        rhs=slot_words[o][:, cols].bitcast(FP8X4),
+                        rhs_scale=slot_scales[4 * o :, cols],
+                        start=(o == 0),
+                        stop=(o == PASSES - 1),
+                    )
+            for j, h in enumerate(halves):
+                nc.scalar.activation(y[h][:, cols], acc[:, j], SILU, bias=bias[:, h, e : e + 1])
 
-        for sort in range(PASSES + 1):
-            gather_tokens(0, sort)
+        for piece in range(S // PIECE):
+            for sort in range(PASSES + 1):
+                gather_tokens(piece, sort)
 
-        per_piece = PIECE // C
-        pending = None
-        for e in range(E):
-            last = e == E - 1
+        def load(e):
             rows = w[e].rearrange("(o p t) n -> p o t n", p=P, t=PACK)
-            if last:
+            if e == E - 1:
                 raw = []
                 for o in range(PASSES):
                     part = stream.tile([P, PACK, N], F32, name="raw")
                     nc.sync.dma_start(part[:], rows[:, o])
                     raw.append(part[:])
-            else:
-                both = stream.tile([P, PASSES, PACK, N], F32, name="raw")
-                nc.sync.dma_start(both[:], rows)
-                raw = [both[:, o] for o in range(PASSES)]
+                return raw
+            both = stream.tile([P, PASSES, PACK, N], F32, name="raw")
+            nc.sync.dma_start(both[:], rows)
+            return [both[:, o] for o in range(PASSES)]
+
+        loaded = {e: load(e) for e in range(BIAS_AFTER + 1)}
+        nc.sync.dma_start(bias[:, :, :E], b.rearrange("(h p) e -> p h e", p=P))
+
+        pending = None
+        for e in range(E):
+            last = e == E - 1
+            raw = loaded[e] if e in loaded else load(e)
             grouped = stage.tile([P, PASSES, N, PACK], BF16, name="grouped", align_bytes=64)
             codes = stage.tile([P, PASSES * N], U32, name="codes", align_bytes=64)
             scales = stage.tile([P, PASSES * N], U8, name="scales", align_bytes=64)
@@ -129,22 +139,21 @@ def tile_moe_pkd_lin_silu_kernel(
                 interleave(nc.scalar.copy, grouped[:, 1], raw[1], P, N)
                 for h in range(HALVES):
                     quantize(codes, scales, grouped, N + h * P, N + (h + 1) * P)
-                    multiply(e, h, codes, scales)
+                    multiply(e, (h,), codes, scales)
             else:
-                interleave(nc.scalar.copy, grouped[:, 1], raw[1], 0, SCALAR_N)
-                interleave(nc.vector.tensor_copy, grouped[:, 1], raw[1], SCALAR_N, N)
+                if e < SCALAR_ALONE:
+                    interleave(nc.scalar.copy, grouped[:, 1], raw[1], 0, N)
+                else:
+                    interleave(nc.scalar.copy, grouped[:, 1], raw[1], 0, SCALAR_N)
+                    interleave(nc.vector.tensor_copy, grouped[:, 1], raw[1], SCALAR_N, N)
                 if pending is not None:
                     pending()
 
                 def finish(e=e, codes=codes, scales=scales, grouped=grouped):
                     quantize(codes, scales, grouped, 0, PASSES * N)
-                    for h in range(HALVES):
-                        multiply(e, h, codes, scales)
+                    multiply(e, (0, 1), codes, scales)
 
                 pending = finish
-                piece, step = divmod(e, per_piece)
-                if piece + 1 < S // PIECE and step <= PASSES:
-                    gather_tokens(piece + 1, step)
 
         token_lists = []
         for r, pos in enumerate((pos1, pos2, pos3, pos4)):
@@ -164,9 +173,9 @@ def tile_moe_pkd_lin_silu_kernel(
 
         cut = T // 2
         for h in range(HALVES):
-            terms = [keep.tile([P, T], F32, name=f"term{h}_{r}") for r in range(TOP)]
-            sum01 = keep.tile([P, T], F32, name=f"sum01_{h}")
-            sum012 = keep.tile([P, T], F32, name=f"sum012_{h}")
+            terms = [keep.tile([P, T], F32, name=f"term{r}") for r in range(TOP)]
+            sum01 = keep.tile([P, T], F32, name="sum01")
+            sum012 = keep.tile([P, T], F32, name="sum012")
             total = keep.tile([P, T], F32, name=f"total{h}")
 
             def fetch(r, t0, t1):

@@ -1,6 +1,7 @@
 from contextlib import ExitStack
 
 import concourse.mybir as mybir
+from concourse.masks import make_identity
 
 K, T, E, C, N = 1024, 640, 20, 128, 256
 TOP = 4
@@ -25,10 +26,11 @@ HALVES = N // P
 WINDOW = 896
 PIECE = 640
 RAW_BUFS = 10
-GROUPED_BUFS = 9
-BIAS_AFTER = 6
-SCALAR_ALONE = 6
-SCALAR_N = 32
+BATCH_BUFS = 9
+BIAS_AFTER = 7
+SCALAR_ALONE = 7
+SPLIT = 3
+WHOLE = E - SPLIT
 
 
 def tile_moe_pkd_lin_silu_kernel(
@@ -38,8 +40,9 @@ def tile_moe_pkd_lin_silu_kernel(
     with ExitStack() as ctx:
         keep = ctx.enter_context(tc.tile_pool(name="keep", bufs=1))
         stream = ctx.enter_context(tc.tile_pool(name="stream", bufs=RAW_BUFS))
-        stage = ctx.enter_context(tc.tile_pool(name="stage", bufs=GROUPED_BUFS))
+        stage = ctx.enter_context(tc.tile_pool(name="stage", bufs=BATCH_BUFS))
         psum = ctx.enter_context(tc.psum_pool(name="psum", bufs=8))
+        scalar_copy, vector_copy = nc.scalar.copy, nc.vector.tensor_copy
 
         slot_list = keep.tile([P, S // 16], U16, name="slot_list")
         nc.sync.dma_start(slot_list[:], offs)
@@ -58,43 +61,78 @@ def tile_moe_pkd_lin_silu_kernel(
                 token_scales[32 * q : 32 * q + 4 * PASSES, : T // 4],
                 x_scales[:, 4 * q : 4 * q + 4, :].bitcast(I32),
             )
-        bias = keep.tile([P, HALVES, 32], F32, name="bias")
 
         slot_words = [keep.tile([P, S], U32, name=f"slot_words{o}", align_bytes=64) for o in range(PASSES)]
         slot_scales = keep.tile([P, S], U8, name="slot_scales", align_bytes=64)
         y = [keep.tile([P, S], F32, name=f"y{h}", align_bytes=64) for h in range(HALVES)]
+        bias = keep.tile([P, HALVES, 32], F32, name="bias")
 
-        def gather_tokens(piece, sort):
+        for piece in range(S // PIECE):
             cols = slice(piece * PIECE, (piece + 1) * PIECE)
             offsets = slot_list[:, piece * PIECE // 16 : (piece + 1) * PIECE // 16]
-            if sort < PASSES:
-                nc.vector.tensor_copy(slot_words[sort][:, cols], token_words[sort][:].bitcast(U32).indirect(offsets))
-            else:
-                nc.vector.tensor_copy(slot_scales[:, cols], token_scales[:].bitcast(U8).indirect(offsets))
+            for o in range(PASSES):
+                vector_copy(slot_words[o][:, cols], token_words[o][:].bitcast(U32).indirect(offsets))
+            vector_copy(slot_scales[:, cols], token_scales[:].bitcast(U8).indirect(offsets))
 
-        def interleave(copy, grouped, raw, n0, n1):
+        def weights(e):
+            return w[e].rearrange("(o p t) n -> p o t n", p=P, t=PACK)
+
+        def load_whole(e):
+            raw = stream.tile([P, PASSES, PACK, N], F32, name="raw")
+            nc.sync.dma_start(raw[:], weights(e))
+            return raw
+
+        def load_half(e, h):
+            raw = stream.tile([P, PASSES, PACK, P], F32, name="raw")
+            for o in range(PASSES):
+                nc.sync.dma_start(raw[:, o], weights(e)[:, o, :, h * P : (h + 1) * P])
+            return raw
+
+        gates = {}
+
+        def load_gates(h, pair):
+            g = stream.tile([P, 2, T], F32, name="raw")
+            nc.sync.dma_start(g[:], gate[2 * pair : 2 * pair + 2, h * P : (h + 1) * P, :].rearrange("r p t -> p r t"))
+            gates[(h, 2 * pair)] = g[:, 0]
+            gates[(h, 2 * pair + 1)] = g[:, 1]
+
+        home = {}
+
+        def new_batch(quarters):
+            width = len(quarters) * P
+            grouped = stage.tile([P, width, PACK], BF16, name="grouped", align_bytes=64)
+            codes = stage.tile([P, width], U32, name="codes", align_bytes=64)
+            scales = stage.tile([P, width], U8, name="scales", align_bytes=64)
+            for place, quarter in enumerate(quarters):
+                home[quarter] = (grouped, codes, scales, place * P)
+
+        def interleave(copy, quarter, source, skip=0):
+            grouped, codes, scales, first = home[quarter]
+            c0 = first + skip
             copy(
-                grouped[:, n0:n1, :].rearrange("p (c i) t -> p c t i", i=4),
-                raw[:, :, n0:n1].rearrange("p t (c i) -> p c t i", i=4),
+                grouped[:, c0 : c0 + source.shape[2], :].rearrange("p (c i) t -> p c t i", i=4),
+                source.rearrange("p t (c i) -> p c t i", i=4),
             )
 
-        def quantize(codes, scales, grouped, lo, hi):
+        def quantize(quarter, count):
+            grouped, codes, scales, lo = home[quarter]
+            hi = lo + count * P
             nc.vector.quantize_mx(
                 out=codes[:, lo:hi].bitcast(FP8X4),
                 scales=scales[:, lo:hi],
-                in_=grouped[:].rearrange("p o n t -> p (o n t)")[:, PACK * lo : PACK * hi],
+                in_=grouped[:, lo:hi, :].rearrange("p n t -> p (n t)"),
             )
 
-        def multiply(e, halves, codes, scales):
+        def multiply(e, halves):
             cols = slice(e * C, (e + 1) * C)
             acc = psum.tile([P, len(halves), C], F32, name="acc")
             for j, h in enumerate(halves):
                 for o in range(PASSES):
-                    m = slice(o * N + h * P, o * N + (h + 1) * P)
+                    grouped, codes, scales, first = home[(e, o, h)]
                     nc.tensor.matmul_mx(
                         out=acc[:, j],
-                        lhsT=codes[:, m].bitcast(FP8X4),
-                        lhsT_scale=scales[:, m],
+                        lhsT=codes[:, first : first + P].bitcast(FP8X4),
+                        lhsT_scale=scales[:, first : first + P],
                         rhs=slot_words[o][:, cols].bitcast(FP8X4),
                         rhs_scale=slot_scales[4 * o :, cols],
                         start=(o == 0),
@@ -103,79 +141,74 @@ def tile_moe_pkd_lin_silu_kernel(
             for j, h in enumerate(halves):
                 nc.scalar.activation(y[h][:, cols], acc[:, j], SILU, bias=bias[:, h, e : e + 1])
 
-        for piece in range(S // PIECE):
-            for sort in range(PASSES + 1):
-                gather_tokens(piece, sort)
-
-        def load(e):
-            rows = w[e].rearrange("(o p t) n -> p o t n", p=P, t=PACK)
-            if e == E - 1:
-                raw = []
-                for o in range(PASSES):
-                    part = stream.tile([P, PACK, N], F32, name="raw")
-                    nc.sync.dma_start(part[:], rows[:, o])
-                    raw.append(part[:])
-                return raw
-            both = stream.tile([P, PASSES, PACK, N], F32, name="raw")
-            nc.sync.dma_start(both[:], rows)
-            return [both[:, o] for o in range(PASSES)]
-
-        loaded = {e: load(e) for e in range(BIAS_AFTER + 1)}
+        loaded = {e: load_whole(e) for e in range(BIAS_AFTER + 1)}
         nc.sync.dma_start(bias[:, :, :E], b.rearrange("(h p) e -> p h e", p=P))
-
-        pending = None
-        for e in range(E):
-            last = e == E - 1
-            raw = loaded[e] if e in loaded else load(e)
-            grouped = stage.tile([P, PASSES, N, PACK], BF16, name="grouped", align_bytes=64)
-            codes = stage.tile([P, PASSES * N], U32, name="codes", align_bytes=64)
-            scales = stage.tile([P, PASSES * N], U8, name="scales", align_bytes=64)
-            interleave(nc.scalar.copy, grouped[:, 0], raw[0], 0, N)
-            if last:
-                if pending is not None:
-                    pending()
-                quantize(codes, scales, grouped, 0, N)
-                interleave(nc.vector.tensor_copy, grouped[:, 1], raw[1], 0, P)
-                interleave(nc.scalar.copy, grouped[:, 1], raw[1], P, N)
-                for h in range(HALVES):
-                    quantize(codes, scales, grouped, N + h * P, N + (h + 1) * P)
-                    multiply(e, (h,), codes, scales)
-            else:
-                if e < SCALAR_ALONE:
-                    interleave(nc.scalar.copy, grouped[:, 1], raw[1], 0, N)
-                else:
-                    interleave(nc.scalar.copy, grouped[:, 1], raw[1], 0, SCALAR_N)
-                    interleave(nc.vector.tensor_copy, grouped[:, 1], raw[1], SCALAR_N, N)
-                if pending is not None:
-                    pending()
-
-                def finish(e=e, codes=codes, scales=scales, grouped=grouped):
-                    quantize(codes, scales, grouped, 0, PASSES * N)
-                    multiply(e, (0, 1), codes, scales)
-
-                pending = finish
-
         token_lists = []
         for r, pos in enumerate((pos1, pos2, pos3, pos4)):
             one = keep.tile([P, T // 16], U16, name=f"token_list{r}")
             nc.sync.dma_start(one[:], pos)
             token_lists.append(one)
 
-        gates = {}
-        for h in range(HALVES):
-            for pair in range(TOP // 2):
-                g = stream.tile([P, 2, T], F32, name="raw")
-                nc.sync.dma_start(
-                    g[:], gate[2 * pair : 2 * pair + 2, h * P : (h + 1) * P, :].rearrange("r p t -> p r t")
-                )
-                gates[(h, 2 * pair)] = g[:, 0]
-                gates[(h, 2 * pair + 1)] = g[:, 1]
+        new_batch([(0, 1, 1)])
+        for e in range(WHOLE):
+            raw = loaded[e] if e in loaded else load_whole(e)
+            lead = (e + 1, 1, 1) if e + 1 < WHOLE else (e + 1, 0, 0)
+            new_batch([(e, 0, 0), (e, 0, 1), (e, 1, 0), lead])
+            second = scalar_copy if e < SCALAR_ALONE else vector_copy
+            interleave(second, (e, 1, 1), raw[:, 1, :, P:])
+            interleave(second, (e, 1, 0), raw[:, 1, :, :P])
+            interleave(scalar_copy, (e, 0, 0), raw[:, 0])
+            if e == 0:
+                quantize((0, 1, 1), 1)
+            else:
+                quantize((e - 1, 0, 0), 4)
+                multiply(e - 1, (0, 1))
 
-        cut = T // 2
+        for e in range(WHOLE, E):
+            raw = load_half(e, 0)
+            if e == WHOLE:
+                new_batch([(e, 1, 0)])
+                interleave(vector_copy, (e, 0, 0), raw[:, 0])
+                interleave(scalar_copy, (e, 1, 0), raw[:, 1])
+                quantize((e - 1, 0, 0), 4)
+                multiply(e - 1, (0, 1))
+                quantize((e, 1, 0), 1)
+            elif e < E - 1:
+                new_batch([(e, 0, 0), (e, 1, 0)])
+                interleave(vector_copy, (e, 0, 0), raw[:, 0])
+                interleave(scalar_copy, (e, 1, 0), raw[:, 1])
+                quantize((e, 0, 0), 2)
+            else:
+                new_batch([(e, 0, 0), (e, 1, 0)])
+                interleave(scalar_copy, (e, 0, 0), raw[:, 0])
+                quantize((e, 0, 0), 1)
+                interleave(vector_copy, (e, 1, 0), raw[:, 1, :, : P // 2])
+                interleave(scalar_copy, (e, 1, 0), raw[:, 1, :, P // 2 :], skip=P // 2)
+                quantize((e, 1, 0), 1)
+            multiply(e, (0,))
+
+        load_gates(0, 0)
+        for e in range(WHOLE, E):
+            if e == E - 1:
+                load_gates(0, 1)
+            raw = load_half(e, 1)
+            new_batch([(e, 0, 1), (e, 1, 1)])
+            for o in range(PASSES):
+                interleave(scalar_copy, (e, o, 1), raw[:, o])
+            quantize((e, 0, 1), 2)
+            multiply(e, (1,))
+        for pair in range(TOP // 2):
+            load_gates(1, pair)
+
+        identity = keep.tile([P, P], F32, name="identity")
+        make_identity(nc, identity[:])
+
+        blocks = T // P
         for h in range(HALVES):
-            terms = [keep.tile([P, T], F32, name=f"term{r}") for r in range(TOP)]
-            sum01 = keep.tile([P, T], F32, name="sum01")
-            sum012 = keep.tile([P, T], F32, name="sum012")
+            last = h == HALVES - 1
+            on_tensor = TOP - 1 if last else TOP
+            terms = [keep.tile([P, T], F32, name=f"term{h}_{r}") for r in range(TOP)]
+            turned = [psum.tile([P, P], F32, name="acc") for j in range(blocks)]
             total = keep.tile([P, T], F32, name=f"total{h}")
 
             def fetch(r, t0, t1):
@@ -186,13 +219,32 @@ def tile_moe_pkd_lin_silu_kernel(
                     MULT,
                 )
 
-            fetch(0, 0, T)
-            fetch(1, 0, T)
-            fetch(2, 0, T)
-            nc.vector.tensor_tensor(sum01[:], terms[0][:], terms[1][:], ADD)
-            fetch(3, 0, cut)
-            nc.vector.tensor_tensor(sum012[:], sum01[:], terms[2][:], ADD)
-            fetch(3, cut, T)
-            for t0, t1 in ((0, cut), (cut, T)):
-                nc.vector.tensor_tensor(total[:, t0:t1], sum012[:, t0:t1], terms[3][:, t0:t1], ADD)
+            spans = ((0, 3 * P), (3 * P, T))
+            for r in range(on_tensor):
+                for t0, t1 in spans if last and r == on_tensor - 1 else ((0, T),):
+                    fetch(r, t0, t1)
+                for j in range(blocks):
+                    nc.tensor.matmul(
+                        turned[j][:],
+                        terms[r][:, j * P : (j + 1) * P],
+                        identity[:],
+                        start=(r == 0),
+                        stop=(r == on_tensor - 1),
+                        is_transpose=True,
+                    )
+            by_token = keep.tile([P, T], F32, name=f"by_token{h}")
+            back = [psum.tile([P, t1 - t0], F32, name="acc") for t0, t1 in spans]
+            for j in range(blocks):
+                nc.scalar.copy(by_token[:, j * P : (j + 1) * P], turned[j][:])
+            for (t0, t1), bank in zip(spans, back):
+                for t in range(t0, t1, P):
+                    nc.tensor.transpose(bank[:, t - t0 : t - t0 + P], by_token[:, t : t + P], identity[:])
+            if last:
+                for t0, t1 in spans:
+                    fetch(TOP - 1, t0, t1)
+            for (t0, t1), bank in zip(spans, back):
+                if last:
+                    nc.vector.tensor_tensor(total[:, t0:t1], terms[TOP - 1][:, t0:t1], bank[:], ADD)
+                else:
+                    nc.scalar.copy(total[:, t0:t1], bank[:])
                 nc.sync.dma_start(out[h * P : (h + 1) * P, t0:t1], total[:, t0:t1])

@@ -23,14 +23,21 @@ P = 128
 PACK = 4
 PASSES = K // (P * PACK)
 HALVES = N // P
-WINDOW = 896
+QUADRANTS = P // 32
+SCALE_ROWS = 4
+LINE = 4
+BANKS = 8
+BIAS_PITCH = 32
+
 PIECE = 640
-RAW_BUFS = 10
-BATCH_BUFS = 9
-BIAS_AFTER = 7
+WINDOW = 896
+STREAM_BUFS = 10
 SCALAR_ALONE = 7
+BIAS_AFTER = 7
+BATCH_BUFS = BIAS_AFTER + 2
 SPLIT = 3
 WHOLE = E - SPLIT
+SPANS = ((0, 3 * P), (3 * P, T))
 
 
 def tile_moe_pkd_lin_silu_kernel(
@@ -39,9 +46,9 @@ def tile_moe_pkd_lin_silu_kernel(
     nc = tc.nc
     with ExitStack() as ctx:
         keep = ctx.enter_context(tc.tile_pool(name="keep", bufs=1))
-        stream = ctx.enter_context(tc.tile_pool(name="stream", bufs=RAW_BUFS))
+        stream = ctx.enter_context(tc.tile_pool(name="stream", bufs=STREAM_BUFS))
         stage = ctx.enter_context(tc.tile_pool(name="stage", bufs=BATCH_BUFS))
-        psum = ctx.enter_context(tc.psum_pool(name="psum", bufs=8))
+        psum = ctx.enter_context(tc.psum_pool(name="psum", bufs=BANKS))
         scalar_copy, vector_copy = nc.scalar.copy, nc.vector.tensor_copy
 
         slot_list = keep.tile([P, S // 16], U16, name="slot_list")
@@ -56,107 +63,106 @@ def tile_moe_pkd_lin_silu_kernel(
 
         token_scales = keep.tile([P, WINDOW // 4], I32, name="token_scales", align_bytes=64)
         nc.vector.memset(token_scales[:], 0)
-        for q in range(4):
+        for q in range(QUADRANTS):
             nc.scalar.dma_start(
-                token_scales[32 * q : 32 * q + 4 * PASSES, : T // 4],
-                x_scales[:, 4 * q : 4 * q + 4, :].bitcast(I32),
+                token_scales[32 * q : 32 * q + SCALE_ROWS * PASSES, : T // 4],
+                x_scales[:, SCALE_ROWS * q : SCALE_ROWS * (q + 1), :].bitcast(I32),
             )
 
         slot_words = [keep.tile([P, S], U32, name=f"slot_words{o}", align_bytes=64) for o in range(PASSES)]
         slot_scales = keep.tile([P, S], U8, name="slot_scales", align_bytes=64)
         y = [keep.tile([P, S], F32, name=f"y{h}", align_bytes=64) for h in range(HALVES)]
-        bias = keep.tile([P, HALVES, 32], F32, name="bias")
+        bias = keep.tile([P, HALVES, BIAS_PITCH], F32, name="bias")
 
         for piece in range(S // PIECE):
-            cols = slice(piece * PIECE, (piece + 1) * PIECE)
+            slots = slice(piece * PIECE, (piece + 1) * PIECE)
             offsets = slot_list[:, piece * PIECE // 16 : (piece + 1) * PIECE // 16]
             for o in range(PASSES):
-                vector_copy(slot_words[o][:, cols], token_words[o][:].bitcast(U32).indirect(offsets))
-            vector_copy(slot_scales[:, cols], token_scales[:].bitcast(U8).indirect(offsets))
+                vector_copy(slot_words[o][:, slots], token_words[o][:].bitcast(U32).indirect(offsets))
+            vector_copy(slot_scales[:, slots], token_scales[:].bitcast(U8).indirect(offsets))
 
         def weights(e):
             return w[e].rearrange("(o p t) n -> p o t n", p=P, t=PACK)
 
         def load_whole(e):
-            raw = stream.tile([P, PASSES, PACK, N], F32, name="raw")
+            raw = stream.tile([P, PASSES, PACK, N], F32, name="streamed")
             nc.sync.dma_start(raw[:], weights(e))
             return raw
 
         def load_half(e, h):
-            raw = stream.tile([P, PASSES, PACK, P], F32, name="raw")
+            raw = stream.tile([P, PASSES, PACK, P], F32, name="streamed")
             for o in range(PASSES):
                 nc.sync.dma_start(raw[:, o], weights(e)[:, o, :, h * P : (h + 1) * P])
             return raw
 
         gates = {}
 
-        def load_gates(h, pair):
-            g = stream.tile([P, 2, T], F32, name="raw")
-            nc.sync.dma_start(g[:], gate[2 * pair : 2 * pair + 2, h * P : (h + 1) * P, :].rearrange("r p t -> p r t"))
-            gates[(h, 2 * pair)] = g[:, 0]
-            gates[(h, 2 * pair + 1)] = g[:, 1]
+        def load_gate(h, r):
+            rows = stream.tile([P, T], F32, name="streamed")
+            nc.sync.dma_start(rows[:], gate[r, h * P : (h + 1) * P, :])
+            gates[(h, r)] = rows[:]
 
         home = {}
 
         def new_batch(quarters):
             width = len(quarters) * P
-            grouped = stage.tile([P, width, PACK], BF16, name="grouped", align_bytes=64)
+            rounded = stage.tile([P, width, PACK], BF16, name="rounded", align_bytes=64)
             codes = stage.tile([P, width], U32, name="codes", align_bytes=64)
             scales = stage.tile([P, width], U8, name="scales", align_bytes=64)
             for place, quarter in enumerate(quarters):
-                home[quarter] = (grouped, codes, scales, place * P)
+                home[quarter] = (rounded, codes, scales, place * P)
 
         def interleave(copy, quarter, source, skip=0):
-            grouped, codes, scales, first = home[quarter]
-            c0 = first + skip
+            rounded, codes, scales, first = home[quarter]
+            columns = slice(first + skip, first + skip + source.shape[2])
             copy(
-                grouped[:, c0 : c0 + source.shape[2], :].rearrange("p (c i) t -> p c t i", i=4),
-                source.rearrange("p t (c i) -> p c t i", i=4),
+                rounded[:, columns, :].rearrange("p (c i) t -> p c t i", i=LINE),
+                source.rearrange("p t (c i) -> p c t i", i=LINE),
             )
 
         def quantize(quarter, count):
-            grouped, codes, scales, lo = home[quarter]
-            hi = lo + count * P
+            rounded, codes, scales, first = home[quarter]
+            columns = slice(first, first + count * P)
             nc.vector.quantize_mx(
-                out=codes[:, lo:hi].bitcast(FP8X4),
-                scales=scales[:, lo:hi],
-                in_=grouped[:, lo:hi, :].rearrange("p n t -> p (n t)"),
+                out=codes[:, columns].bitcast(FP8X4),
+                scales=scales[:, columns],
+                in_=rounded[:, columns, :].rearrange("p n t -> p (n t)"),
             )
 
         def multiply(e, halves):
-            cols = slice(e * C, (e + 1) * C)
-            acc = psum.tile([P, len(halves), C], F32, name="acc")
+            slots = slice(e * C, (e + 1) * C)
+            sums = psum.tile([P, len(halves), C], F32, name="bank")
             for j, h in enumerate(halves):
                 for o in range(PASSES):
-                    grouped, codes, scales, first = home[(e, o, h)]
+                    rounded, codes, scales, first = home[(e, o, h)]
                     nc.tensor.matmul_mx(
-                        out=acc[:, j],
+                        out=sums[:, j],
                         lhsT=codes[:, first : first + P].bitcast(FP8X4),
                         lhsT_scale=scales[:, first : first + P],
-                        rhs=slot_words[o][:, cols].bitcast(FP8X4),
-                        rhs_scale=slot_scales[4 * o :, cols],
+                        rhs=slot_words[o][:, slots].bitcast(FP8X4),
+                        rhs_scale=slot_scales[SCALE_ROWS * o :, slots],
                         start=(o == 0),
                         stop=(o == PASSES - 1),
                     )
             for j, h in enumerate(halves):
-                nc.scalar.activation(y[h][:, cols], acc[:, j], SILU, bias=bias[:, h, e : e + 1])
+                nc.scalar.activation(y[h][:, slots], sums[:, j], SILU, bias=bias[:, h, e : e + 1])
 
         loaded = {e: load_whole(e) for e in range(BIAS_AFTER + 1)}
         nc.sync.dma_start(bias[:, :, :E], b.rearrange("(h p) e -> p h e", p=P))
         token_lists = []
         for r, pos in enumerate((pos1, pos2, pos3, pos4)):
-            one = keep.tile([P, T // 16], U16, name=f"token_list{r}")
-            nc.sync.dma_start(one[:], pos)
-            token_lists.append(one)
+            token_list = keep.tile([P, T // 16], U16, name=f"token_list{r}")
+            nc.sync.dma_start(token_list[:], pos)
+            token_lists.append(token_list)
 
         new_batch([(0, 1, 1)])
         for e in range(WHOLE):
             raw = loaded[e] if e in loaded else load_whole(e)
-            lead = (e + 1, 1, 1) if e + 1 < WHOLE else (e + 1, 0, 0)
-            new_batch([(e, 0, 0), (e, 0, 1), (e, 1, 0), lead])
-            second = scalar_copy if e < SCALAR_ALONE else vector_copy
-            interleave(second, (e, 1, 1), raw[:, 1, :, P:])
-            interleave(second, (e, 1, 0), raw[:, 1, :, :P])
+            ahead = (e + 1, 1, 1) if e + 1 < WHOLE else (e + 1, 0, 0)
+            new_batch([(e, 0, 0), (e, 0, 1), (e, 1, 0), ahead])
+            pass1_copy = scalar_copy if e < SCALAR_ALONE else vector_copy
+            interleave(pass1_copy, (e, 1, 1), raw[:, 1, :, P:])
+            interleave(pass1_copy, (e, 1, 0), raw[:, 1, :, :P])
             interleave(scalar_copy, (e, 0, 0), raw[:, 0])
             if e == 0:
                 quantize((0, 1, 1), 1)
@@ -187,28 +193,28 @@ def tile_moe_pkd_lin_silu_kernel(
                 quantize((e, 1, 0), 1)
             multiply(e, (0,))
 
-        load_gates(0, 0)
-        for e in range(WHOLE, E):
-            if e == E - 1:
-                load_gates(0, 1)
+        for r, e in enumerate(range(WHOLE, E)):
+            load_gate(0, r)
             raw = load_half(e, 1)
             new_batch([(e, 0, 1), (e, 1, 1)])
             for o in range(PASSES):
                 interleave(scalar_copy, (e, o, 1), raw[:, o])
             quantize((e, 0, 1), 2)
             multiply(e, (1,))
-        for pair in range(TOP // 2):
-            load_gates(1, pair)
+        load_gate(1, 0)
+        load_gate(0, TOP - 1)
+        for r in range(1, TOP):
+            load_gate(1, r)
 
         identity = keep.tile([P, P], F32, name="identity")
         make_identity(nc, identity[:])
 
         blocks = T // P
         for h in range(HALVES):
-            last = h == HALVES - 1
-            on_tensor = TOP - 1 if last else TOP
+            last_half = h == HALVES - 1
+            on_tensor = TOP - 1 if last_half else TOP
             terms = [keep.tile([P, T], F32, name=f"term{h}_{r}") for r in range(TOP)]
-            turned = [psum.tile([P, P], F32, name="acc") for j in range(blocks)]
+            turned = [psum.tile([P, P], F32, name="bank") for j in range(blocks)]
             total = keep.tile([P, T], F32, name=f"total{h}")
 
             def fetch(r, t0, t1):
@@ -219,9 +225,8 @@ def tile_moe_pkd_lin_silu_kernel(
                     MULT,
                 )
 
-            spans = ((0, 3 * P), (3 * P, T))
             for r in range(on_tensor):
-                for t0, t1 in spans if last and r == on_tensor - 1 else ((0, T),):
+                for t0, t1 in SPANS if last_half and r == on_tensor - 1 else ((0, T),):
                     fetch(r, t0, t1)
                 for j in range(blocks):
                     nc.tensor.matmul(
@@ -233,17 +238,17 @@ def tile_moe_pkd_lin_silu_kernel(
                         is_transpose=True,
                     )
             by_token = keep.tile([P, T], F32, name=f"by_token{h}")
-            back = [psum.tile([P, t1 - t0], F32, name="acc") for t0, t1 in spans]
+            back = [psum.tile([P, t1 - t0], F32, name="bank") for t0, t1 in SPANS]
             for j in range(blocks):
                 nc.scalar.copy(by_token[:, j * P : (j + 1) * P], turned[j][:])
-            for (t0, t1), bank in zip(spans, back):
+            for (t0, t1), bank in zip(SPANS, back):
                 for t in range(t0, t1, P):
                     nc.tensor.transpose(bank[:, t - t0 : t - t0 + P], by_token[:, t : t + P], identity[:])
-            if last:
-                for t0, t1 in spans:
+            if last_half:
+                for t0, t1 in SPANS:
                     fetch(TOP - 1, t0, t1)
-            for (t0, t1), bank in zip(spans, back):
-                if last:
+            for (t0, t1), bank in zip(SPANS, back):
+                if last_half:
                     nc.vector.tensor_tensor(total[:, t0:t1], terms[TOP - 1][:, t0:t1], bank[:], ADD)
                 else:
                     nc.scalar.copy(total[:, t0:t1], bank[:])

from contextlib import ExitStack

import concourse.mybir as mybir
from concourse.masks import make_identity

K, T, E, C, N = 1024, 640, 20, 128, 256
TOP = 4
S = E * C
FLOPS = 2 * S * K * N

F32 = mybir.dt.float32
BF16 = mybir.dt.bfloat16
I32 = mybir.dt.int32
U32 = mybir.dt.uint32
U16 = mybir.dt.uint16
U8 = mybir.dt.uint8
FP8X4 = mybir.dt.float8_e4m3fn_x4
MULT = mybir.AluOpType.mult
ADD = mybir.AluOpType.add
SILU = mybir.ActivationFunctionType.Silu

P = 128
PACK = 4
PASSES = K // (P * PACK)
HALVES = N // P
QUADRANTS = P // 32
SCALE_ROWS = 4
LINE = 4
BANKS = 8
BIAS_PITCH = 32

PIECE = 640
WINDOW = 896
STREAM_BUFS = 10
SCALAR_ALONE = 7
BIAS_AFTER = 7
BATCH_BUFS = BIAS_AFTER + 2
SPLIT = 3
WHOLE = E - SPLIT
SPANS = ((0, 3 * P), (3 * P, T))


def tile_moe_pkd_lin_silu_kernel(
    tc, x_words, x_scales, w, b, gate, offs, pos1, pos2, pos3, pos4, out
):
    nc = tc.nc
    with ExitStack() as ctx:
        keep = ctx.enter_context(tc.tile_pool(name="keep", bufs=1))
        stream = ctx.enter_context(tc.tile_pool(name="stream", bufs=STREAM_BUFS))
        stage = ctx.enter_context(tc.tile_pool(name="stage", bufs=BATCH_BUFS))
        psum = ctx.enter_context(tc.psum_pool(name="psum", bufs=BANKS))
        scalar_copy, vector_copy = nc.scalar.copy, nc.vector.tensor_copy

        slot_list = keep.tile([P, S // 16], U16, name="slot_list")
        nc.sync.dma_start(slot_list[:], offs)

        token_words = []
        for o in range(PASSES):
            words = keep.tile([P, WINDOW], I32, name=f"token_words{o}", align_bytes=64)
            nc.vector.memset(words[:, T:], 0)
            nc.sync.dma_start(words[:, :T], x_words[o].rearrange("p t r -> p (t r)").bitcast(I32))
            token_words.append(words)

        token_scales = keep.tile([P, WINDOW // 4], I32, name="token_scales", align_bytes=64)
        nc.vector.memset(token_scales[:], 0)
        for q in range(QUADRANTS):
            nc.scalar.dma_start(
                token_scales[32 * q : 32 * q + SCALE_ROWS * PASSES, : T // 4],
                x_scales[:, SCALE_ROWS * q : SCALE_ROWS * (q + 1), :].bitcast(I32),
            )

        slot_words = [keep.tile([P, S], U32, name=f"slot_words{o}", align_bytes=64) for o in range(PASSES)]
        slot_scales = keep.tile([P, S], U8, name="slot_scales", align_bytes=64)
        y = [keep.tile([P, S], F32, name=f"y{h}", align_bytes=64) for h in range(HALVES)]
        bias = keep.tile([P, HALVES, BIAS_PITCH], F32, name="bias")

        for piece in range(S // PIECE):
            slots = slice(piece * PIECE, (piece + 1) * PIECE)
            offsets = slot_list[:, piece * PIECE // 16 : (piece + 1) * PIECE // 16]
            for o in range(PASSES):
                vector_copy(slot_words[o][:, slots], token_words[o][:].bitcast(U32).indirect(offsets))
            vector_copy(slot_scales[:, slots], token_scales[:].bitcast(U8).indirect(offsets))

        def weights(e):
            return w[e].rearrange("(o p t) n -> p o t n", p=P, t=PACK)

        def load_whole(e):
            raw = stream.tile([P, PASSES, PACK, N], F32, name="streamed")
            nc.sync.dma_start(raw[:], weights(e))
            return raw

        def load_half(e, h):
            raw = stream.tile([P, PASSES, PACK, P], F32, name="streamed")
            for o in range(PASSES):
                nc.sync.dma_start(raw[:, o], weights(e)[:, o, :, h * P : (h + 1) * P])
            return raw

        gates = {}

        def load_gate(h, r):
            rows = stream.tile([P, T], F32, name="streamed")
            nc.sync.dma_start(rows[:], gate[r, h * P : (h + 1) * P, :])
            gates[(h, r)] = rows[:]

        home = {}

        def new_batch(quarters):
            width = len(quarters) * P
            rounded = stage.tile([P, width, PACK], BF16, name="rounded", align_bytes=64)
            codes = stage.tile([P, width], U32, name="codes", align_bytes=64)
            scales = stage.tile([P, width], U8, name="scales", align_bytes=64)
            for place, quarter in enumerate(quarters):
                home[quarter] = (rounded, codes, scales, place * P)

        def interleave(copy, quarter, source, skip=0):
            rounded, codes, scales, first = home[quarter]
            columns = slice(first + skip, first + skip + source.shape[2])
            copy(
                rounded[:, columns, :].rearrange("p (c i) t -> p c t i", i=LINE),
                source.rearrange("p t (c i) -> p c t i", i=LINE),
            )

        def quantize(quarter, count):
            rounded, codes, scales, first = home[quarter]
            columns = slice(first, first + count * P)
            nc.vector.quantize_mx(
                out=codes[:, columns].bitcast(FP8X4),
                scales=scales[:, columns],
                in_=rounded[:, columns, :].rearrange("p n t -> p (n t)"),
            )

        def multiply(e, halves):
            slots = slice(e * C, (e + 1) * C)
            sums = psum.tile([P, len(halves), C], F32, name="bank")
            for j, h in enumerate(halves):
                for o in range(PASSES):
                    rounded, codes, scales, first = home[(e, o, h)]
                    nc.tensor.matmul_mx(
                        out=sums[:, j],
                        lhsT=codes[:, first : first + P].bitcast(FP8X4),
                        lhsT_scale=scales[:, first : first + P],
                        rhs=slot_words[o][:, slots].bitcast(FP8X4),
                        rhs_scale=slot_scales[SCALE_ROWS * o :, slots],
                        start=(o == 0),
                        stop=(o == PASSES - 1),
                    )
            for j, h in enumerate(halves):
                nc.scalar.activation(y[h][:, slots], sums[:, j], SILU, bias=bias[:, h, e : e + 1])

        loaded = {e: load_whole(e) for e in range(BIAS_AFTER + 1)}
        nc.sync.dma_start(bias[:, :, :E], b.rearrange("(h p) e -> p h e", p=P))
        token_lists = []
        for r, pos in enumerate((pos1, pos2, pos3, pos4)):
            token_list = keep.tile([P, T // 16], U16, name=f"token_list{r}")
            nc.sync.dma_start(token_list[:], pos)
            token_lists.append(token_list)

        new_batch([(0, 1, 1)])
        for e in range(WHOLE):
            raw = loaded[e] if e in loaded else load_whole(e)
            ahead = (e + 1, 1, 1) if e + 1 < WHOLE else (e + 1, 0, 0)
            new_batch([(e, 0, 0), (e, 0, 1), (e, 1, 0), ahead])
            pass1_copy = scalar_copy if e < SCALAR_ALONE else vector_copy
            interleave(pass1_copy, (e, 1, 1), raw[:, 1, :, P:])
            interleave(pass1_copy, (e, 1, 0), raw[:, 1, :, :P])
            interleave(scalar_copy, (e, 0, 0), raw[:, 0])
            if e == 0:
                quantize((0, 1, 1), 1)
            else:
                quantize((e - 1, 0, 0), 4)
                multiply(e - 1, (0, 1))

        for e in range(WHOLE, E):
            raw = load_half(e, 0)
            if e == WHOLE:
                new_batch([(e, 1, 0)])
                interleave(vector_copy, (e, 0, 0), raw[:, 0])
                interleave(scalar_copy, (e, 1, 0), raw[:, 1])
                quantize((e - 1, 0, 0), 4)
                multiply(e - 1, (0, 1))
                quantize((e, 1, 0), 1)
            elif e < E - 1:
                new_batch([(e, 0, 0), (e, 1, 0)])
                interleave(vector_copy, (e, 0, 0), raw[:, 0])
                interleave(scalar_copy, (e, 1, 0), raw[:, 1])
                quantize((e, 0, 0), 2)
            else:
                new_batch([(e, 0, 0), (e, 1, 0)])
                interleave(scalar_copy, (e, 0, 0), raw[:, 0])
                quantize((e, 0, 0), 1)
                interleave(vector_copy, (e, 1, 0), raw[:, 1, :, : P // 2])
                interleave(scalar_copy, (e, 1, 0), raw[:, 1, :, P // 2 :], skip=P // 2)
                quantize((e, 1, 0), 1)
            multiply(e, (0,))

        for r, e in enumerate(range(WHOLE, E)):
            load_gate(0, r)
            raw = load_half(e, 1)
            new_batch([(e, 0, 1), (e, 1, 1)])
            for o in range(PASSES):
                interleave(scalar_copy, (e, o, 1), raw[:, o])
            quantize((e, 0, 1), 2)
            multiply(e, (1,))
        load_gate(1, 0)
        load_gate(0, TOP - 1)
        for r in range(1, TOP):
            load_gate(1, r)

        identity = keep.tile([P, P], F32, name="identity")
        make_identity(nc, identity[:])

        blocks = T // P
        for h in range(HALVES):
            last_half = h == HALVES - 1
            on_tensor = TOP - 1 if last_half else TOP
            terms = [keep.tile([P, T], F32, name=f"term{h}_{r}") for r in range(TOP)]
            turned = [psum.tile([P, P], F32, name="bank") for j in range(blocks)]
            total = keep.tile([P, T], F32, name=f"total{h}")

            def fetch(r, t0, t1):
                nc.vector.tensor_tensor(
                    terms[r][:, t0:t1],
                    y[h][:].indirect(token_lists[r][:, t0 // 16 : t1 // 16]),
                    gates[(h, r)][:, t0:t1],
                    MULT,
                )

            for r in range(on_tensor):
                for t0, t1 in SPANS if last_half and r == on_tensor - 1 else ((0, T),):
                    fetch(r, t0, t1)
                for j in range(blocks):
                    nc.tensor.matmul(
                        turned[j][:],
                        terms[r][:, j * P : (j + 1) * P],
                        identity[:],
                        start=(r == 0),
                        stop=(r == on_tensor - 1),
                        is_transpose=True,
                    )
            by_token = keep.tile([P, T], F32, name=f"by_token{h}")
            back = [psum.tile([P, t1 - t0], F32, name="bank") for t0, t1 in SPANS]
            for j in range(blocks):
                nc.scalar.copy(by_token[:, j * P : (j + 1) * P], turned[j][:])
            for (t0, t1), bank in zip(SPANS, back):
                for t in range(t0, t1, P):
                    nc.tensor.transpose(bank[:, t - t0 : t - t0 + P], by_token[:, t : t + P], identity[:])
            if last_half:
                for t0, t1 in SPANS:
                    fetch(TOP - 1, t0, t1)
            for (t0, t1), bank in zip(SPANS, back):
                if last_half:
                    nc.vector.tensor_tensor(total[:, t0:t1], terms[TOP - 1][:, t0:t1], bank[:], ADD)
                else:
                    nc.scalar.copy(total[:, t0:t1], bank[:])
                nc.sync.dma_start(out[h * P : (h + 1) * P, t0:t1], total[:, t0:t1])
